import numpy as np
import ml_dtypes


def mxq(x, axis, fmt="e4m3"):
    dtype, down = {"e4m3": (ml_dtypes.float8_e4m3fn, 7), "e5m2": (ml_dtypes.float8_e5m2, 14)}[fmt]
    v = np.moveaxis(np.asarray(x, np.float32).astype(ml_dtypes.bfloat16).astype(np.float64), axis, -1)
    blocks = v.reshape(v.shape[:-1] + (-1, 32))
    amax = np.abs(blocks).max(-1, keepdims=True)
    byte = np.maximum(np.where(amax > 0, np.frexp(amax)[1] - 1 + 127, 0) - down, 1)
    scale = np.exp2(byte - 127.0)
    codes = (blocks / scale).astype(np.float32).astype(dtype).astype(np.float64)
    return np.moveaxis((codes * scale).reshape(v.shape), -1, axis)


WIDE = False


def mx_kscale(k):
    if not WIDE:
        return np.ones(k)
    levels = np.array([10, -10, 5, -5, 0])
    if k % 512:
        return np.exp2(np.random.permutation(np.resize(levels, k // 32))).repeat(32)
    a = np.empty((k // 512, 16))
    for p in range(k // 512):
        a[p, :8] = np.random.permutation(np.resize(levels, 8))
        for g in range(8):
            far = levels[np.abs(levels - a[p, g]) >= 10]
            a[p, g + 8] = far[np.random.randint(len(far))]
    return np.exp2(a.ravel()).repeat(32)


def f64(x):
    return np.asarray(x).astype(np.float64)


def striped(idx):
    return np.tile(idx.reshape(-1, 16).T, (8, 1)).astype(np.uint16)


def unstriped(offs):
    return offs[:16].T.reshape(-1).astype(np.int64)


def pack_weight(w):
    k, n = w.shape
    w = f64(np.asarray(w, np.float32).astype(ml_dtypes.bfloat16)).reshape(k // 32, 32, n)
    amax = np.abs(w).max(1)
    byte = np.clip(np.where(amax > 0, np.frexp(amax)[1] - 1 + 127 - 7, 1), 1, 254)
    scaled = (w * np.exp2(127.0 - byte)[:, None, :]).reshape(k, n).astype(np.float32)
    words = np.ascontiguousarray(scaled.reshape(k // 512, 128, 4, n).transpose(0, 1, 3, 2)).astype(ml_dtypes.float8_e4m3fn).view(np.uint8)
    return words, np.ascontiguousarray(byte.astype(np.uint8).reshape(k // 512, 16, n))


def unpack_weight(words, scales):
    g, p, n, _ = words.shape
    vals = np.ascontiguousarray(words).view(ml_dtypes.float8_e4m3fn).astype(np.float64) * np.repeat(np.exp2(scales.astype(np.float64) - 127.0), 8, axis=1)[..., None]
    return vals.transpose(0, 1, 3, 2).reshape(g * 512, n)


K, T, S, N, H = 512, 2048, 512, 128, 512


def setup_inputs():
    n = np.random.standard_normal
    s = mx_kscale(K)[:, None]
    u = mx_kscale(H)
    packed_xT = pack_weight(n((K, T)) * s)
    return {
        "x_words": packed_xT[0],
        "x_scales": packed_xT[1],
        "hT": (n((K, H)) / np.sqrt(K) / s).astype(np.float32),
        "unit": (np.random.uniform(0.6, 1.4, (H, 1)) * u[:, None]).astype(np.float32),
        "w1": (n((H, N)) / np.sqrt(H) / u[:, None]).astype(np.float32),
        "offs": striped(np.random.permutation(T)[:S]),
        "cit": striped(np.random.permutation(S)),
    }


def reference(x_words, x_scales, hT, unit, w1, offs, cit):
    hTq = mxq(f64(hT), 0, "e4m3")
    xq = unpack_weight(x_words, x_scales)[:, unstriped(offs)]
    y = hTq.T @ xq
    ker = np.exp(1.2 * np.tanh(y))
    pop = ker.mean(axis=1, keepdims=True)
    cal = ker / (pop + 0.3)
    zc = cal[:, unstriped(cit)]
    prop = cal + 0.6 * zc
    hid = f64(unit) * (prop - (0.5 * ker[:, unstriped(cit)]))
    return mxq(f64(w1), 0, "e4m3").T @ mxq(hid, 0, "e4m3")

from contextlib import ExitStack

import concourse.mybir as mybir

K, T, S, N, H = 512, 2048, 512, 128, 512
FLOPS = 2 * K * H * S + 2 * H * N * S

F32 = mybir.dt.float32
BF16 = mybir.dt.bfloat16
I32 = mybir.dt.int32
U32 = mybir.dt.uint32
U16 = mybir.dt.uint16
U8 = mybir.dt.uint8
FP8X4 = mybir.dt.float8_e4m3fn_x4
ALU = mybir.AluOpType
ACT = mybir.ActivationFunctionType

P = 128
PACK = 4
LISTW = 16


def tile_picked_yanchr_lin_p_kernel(tc, x_words, x_scales, hT, unit, w1, offs, cit, out):
    nc = tc.nc
    with ExitStack() as ctx:
        keep = ctx.enter_context(tc.tile_pool(name="keep", bufs=1))
        psum = ctx.enter_context(tc.psum_pool(name="psum", bufs=1))

        offs_sb = keep.tile([P, S // LISTW], U16, name="offs_sb")
        cit_sb = keep.tile([P, S // LISTW], U16, name="cit_sb")
        x_tab = keep.tile([P, T], U32, name="x_tab", align_bytes=64)
        s_tab = keep.tile([P, T], U8, name="s_tab", align_bytes=64)
        h_raw = [keep.tile([P, PACK, H // 2], F32, name=f"h_raw{b}", align_bytes=64) for b in range(2)]
        w_raw = keep.tile([P, PACK, N], F32, name="w_raw", align_bytes=64)
        unit_sb = keep.tile([P, PACK], F32, name="unit_sb")

        nc.gpsimd.memset(s_tab[:].bitcast(I32), 0)
        nc.sync.dma_start(out=offs_sb[:], in_=offs)
        h_rows = hT.rearrange("(p j) c -> p j c", j=PACK)
        for b in range(2):
            nc.sync.dma_start(out=h_raw[b][:], in_=h_rows[:, :, b * (H // 2) : (b + 1) * (H // 2)])
        for q in range(4):
            nc.sync.dma_start(out=s_tab[32 * q : 32 * q + 4, :].bitcast(I32), in_=x_scales[0, 4 * q : 4 * q + 4, :].bitcast(I32))
        nc.sync.dma_start(out=x_tab[:].bitcast(I32), in_=x_words[0].rearrange("p n t -> p (n t)").bitcast(I32))
        nc.sync.dma_start(out=w_raw[:], in_=w1.rearrange("(p j) n -> p j n", j=PACK))
        nc.sync.dma_start(out=cit_sb[:], in_=cit)
        nc.sync.dma_start(out=unit_sb[:], in_=unit.rearrange("(p t) o -> p (t o)", t=PACK))

        xg_scales = keep.tile([P, S], U8, name="xg_scales", align_bytes=64)
        nc.vector.tensor_copy(out=xg_scales[:], in_=s_tab[:].indirect(offs_sb[:]))

        h_bf = keep.tile([P, PACK, P, PACK], BF16, name="h_bf", align_bytes=64)
        for b in range(2):
            src = h_raw[b][:].rearrange("p j (m t) -> p m t j", t=PACK)
            dst = h_bf[:, :, b * (P // 2) : (b + 1) * (P // 2), :].rearrange("p t m j -> p m t j")
            if b == 0:
                nc.vector.tensor_copy(out=dst, in_=src)
            else:
                nc.scalar.copy(out=dst, in_=src)
        h_all = keep.tile([P, H], U32, name="h_all", align_bytes=64)
        h_sc = keep.tile([P, H], U8, name="h_sc", align_bytes=64)
        nc.vector.quantize_mx(out=h_all[:].bitcast(FP8X4), scales=h_sc[:], in_=h_bf[:].rearrange("p t m j -> p (t m j)"))
        h_codes = [h_all[:, t * P : (t + 1) * P] for t in range(PACK)]
        h_scales = [h_sc[:, t * P : (t + 1) * P] for t in range(PACK)]

        xg_words = keep.tile([P, S], U32, name="xg_words", align_bytes=64)
        nc.vector.tensor_copy(out=xg_words[:], in_=x_tab[:].indirect(offs_sb[:]))

        w_bf = keep.tile([P, N, PACK], BF16, name="w_bf", align_bytes=64)
        nc.vector.tensor_copy(
            out=w_bf[:].rearrange("p (c i) j -> p c j i", i=4), in_=w_raw[:].rearrange("p j (c i) -> p c j i", i=4)
        )
        w_codes = keep.tile([P, N], U32, name="w_codes", align_bytes=64)
        w_scales = keep.tile([P, N], U8, name="w_scales", align_bytes=64)
        nc.vector.quantize_mx(out=w_codes[:].bitcast(FP8X4), scales=w_scales[:], in_=w_bf[:].rearrange("p n j -> p (n j)"))

        sums = keep.tile([P, PACK], F32, name="sums")
        coef = keep.tile([P, PACK], F32, name="coef")
        kers = []
        for t in range(PACK):
            y = psum.tile([P, S], F32, name=f"y{t}")
            nc.tensor.matmul_mx(
                out=y[:], lhsT=h_codes[t].bitcast(FP8X4), lhsT_scale=h_scales[t],
                rhs=xg_words[:].bitcast(FP8X4), rhs_scale=xg_scales[:], start=True, stop=True,
            )
            th = keep.tile([P, S], F32, name=f"th{t}", tag=f"th{t}", align_bytes=64)
            nc.scalar.activation(out=th[:], in_=y[:], func=ACT.Tanh)
            ker = keep.tile([P, S], F32, name=f"ker{t}", align_bytes=64)
            nc.scalar.activation(out=ker[:], in_=th[:], func=ACT.Exp, scale=1.2, accum_out=sums[:, t : t + 1])
            nc.vector.tensor_scalar(
                out=coef[:, t : t + 1], in0=sums[:, t : t + 1], scalar1=-0.5 / S, scalar2=0.6 - 0.5 * 0.3, op0=ALU.mult, op1=ALU.add
            )
            kers.append(ker)

        bounds = [0,128,256,384,512]
        first_scalar = [3,2,1,0]
        nch = len(bounds) - 1
        cited = {}
        for t in range(PACK):
            n = bounds[first_scalar[t]]
            if n > 0:
                got = keep.tile([P, n], F32, name=f"got{t}", align_bytes=64)
                nc.vector.tensor_copy(out=got[:], in_=kers[t][:].indirect(cit_sb[:, 0 : n // LISTW]))
                for c in range(first_scalar[t]):
                    cited[t, c] = got[:, bounds[c] : bounds[c + 1]]
        late = keep.tile([P, sum(S - bounds[f] for f in first_scalar)], F32, name="late", tag=f"th{PACK - 1}", align_bytes=64)
        at = 0
        for c in range(nch):
            for t in reversed(range(PACK)):
                if c >= first_scalar[t]:
                    width = bounds[c + 1] - bounds[c]
                    cited[t, c] = late[:, at : at + width]
                    at = at + width
                    nc.scalar.activation(out=cited[t, c], in_=kers[t][:].indirect(cit_sb[:, bounds[c] // LISTW : bounds[c + 1] // LISTW]), func=ACT.Copy)

        den = keep.tile([P, PACK], F32, name="den")
        nc.vector.tensor_scalar(out=den[:], in0=sums[:], scalar1=1.0 / S, scalar2=0.3, op0=ALU.mult, op1=ALU.add)
        inv = keep.tile([P, PACK], F32, name="inv")
        nc.vector.reciprocal(out=inv[:], in_=den[:])
        gain = keep.tile([P, PACK], F32, name="gain")
        nc.vector.tensor_tensor(out=gain[:], in0=inv[:], in1=unit_sb[:], op=ALU.mult)

        mix = []
        for c in range(nch):
            width = bounds[c + 1] - bounds[c]
            cols = slice(bounds[c], bounds[c + 1])
            mix.append(keep.tile([P, PACK, width], F32, name=f"mix{c}", align_bytes=64))
            for t in range(PACK):
                nc.vector.scalar_tensor_tensor(
                    out=mix[c][:, t, :], in0=cited[t, c], scalar=coef[:, t : t + 1], in1=kers[t][:, cols], op0=ALU.mult, op1=ALU.add
                )
            hid = keep.tile([P, width, PACK], BF16, name=f"hid{c}", align_bytes=64)
            nc.vector.tensor_tensor(
                out=hid[:].rearrange("p (g i) t -> p g t i", i=4),
                in0=mix[c][:].rearrange("p t (g i) -> p g t i", i=4),
                in1=gain[:].unsqueeze(1).unsqueeze(3).to_broadcast([P, width // 4, PACK, 4]),
                op=ALU.mult,
            )
            g_codes = keep.tile([P, width], U32, name=f"g_codes{c}", align_bytes=64)
            g_scales = keep.tile([P, width], U8, name=f"g_scales{c}", align_bytes=64)
            nc.vector.quantize_mx(out=g_codes[:].bitcast(FP8X4), scales=g_scales[:], in_=hid[:].rearrange("p n t -> p (n t)"))
            acc = psum.tile([P, width], F32, name=f"acc{c}")
            nc.tensor.matmul_mx(
                out=acc[:], lhsT=w_codes[:].bitcast(FP8X4), lhsT_scale=w_scales[:],
                rhs=g_codes[:].bitcast(FP8X4), rhs_scale=g_scales[:], start=True, stop=True,
            )
            res = keep.tile([P, width], F32, name=f"res{c}", align_bytes=64)
            nc.scalar.copy(out=res[:], in_=acc[:])
            nc.sync.dma_start(out=out[:, cols], in_=res[:])
